import numpy as np
import ml_dtypes


def mxq(x, axis, fmt="e4m3"):
    dtype, down = {"e4m3": (ml_dtypes.float8_e4m3fn, 7), "e5m2": (ml_dtypes.float8_e5m2, 14)}[fmt]
    v = np.moveaxis(np.asarray(x, np.float32).astype(ml_dtypes.bfloat16).astype(np.float64), axis, -1)
    blocks = v.reshape(v.shape[:-1] + (-1, 32))
    amax = np.abs(blocks).max(-1, keepdims=True)
    byte = np.maximum(np.where(amax > 0, np.frexp(amax)[1] - 1 + 127, 0) - down, 1)
    scale = np.exp2(byte - 127.0)
    codes = (blocks / scale).astype(np.float32).astype(dtype).astype(np.float64)
    return np.moveaxis((codes * scale).reshape(v.shape), -1, axis)


WIDE = False


def mx_kscale(k):
    if not WIDE:
        return np.ones(k)
    levels = np.array([30, -30])
    if k % 512:
        return np.exp2(np.random.permutation(np.resize(levels, k // 32))).repeat(32)
    a = np.empty((k // 512, 16))
    for p in range(k // 512):
        a[p, :8] = np.random.permutation(np.resize(levels, 8))
        for g in range(8):
            far = levels[np.abs(levels - a[p, g]) >= 10]
            a[p, g + 8] = far[np.random.randint(len(far))]
    return np.exp2(a.ravel()).repeat(32)


def f64(x):
    return np.asarray(x).astype(np.float64)


def striped(idx):
    return np.tile(np.asarray(idx).reshape(-1, 16).T, (8, 1)).astype(np.uint16)


def unstriped(offs):
    return offs[:16].T.reshape(-1).astype(np.int64)


E2M1 = np.array([0.0, 0.5, 1.0, 1.5, 2.0, 3.0, 4.0, 6.0, -0.0, -0.5, -1.0, -1.5, -2.0, -3.0, -4.0, -6.0])


def pack_weight(w, fmt):
    k, n = w.shape
    w = f64(np.asarray(w, np.float32).astype(ml_dtypes.bfloat16)).reshape(k // 32, 32, n)
    amax = np.abs(w).max(1)
    if fmt in ("e4m3", "e5m2"):
        byte = np.frexp(amax)[1] - 1 + 127 - (7 if fmt == "e4m3" else 14)
    else:
        mant, ex = np.frexp(amax / 6.0)
        byte = np.where(mant > 0.5, ex, ex - 1) + 127
    byte = np.clip(np.where(amax > 0, byte, 1), 1, 254)
    scaled = (w * np.exp2(127.0 - byte)[:, None, :]).reshape(k, n).astype(np.float32)
    by_word = np.ascontiguousarray(scaled.reshape(k // 512, 128, 4, n).transpose(0, 1, 3, 2))
    if fmt in ("e4m3", "e5m2"):
        words = by_word.astype(ml_dtypes.float8_e4m3fn if fmt == "e4m3" else ml_dtypes.float8_e5m2).view(np.uint8)
    else:
        c = by_word.astype(ml_dtypes.float4_e2m1fn).view(np.uint8) & 0xF
        words = (c[..., 0::2] | (c[..., 1::2] << 4)).reshape(k // 512, 128, 2 * n)
    return np.ascontiguousarray(words), np.ascontiguousarray(byte.astype(np.uint8).reshape(k // 512, 16, n))


def unpack_weight(words, scales, fmt):
    g, _, n = scales.shape
    words = np.ascontiguousarray(words).reshape(g, 128, n, -1)
    if fmt in ("e4m3", "e5m2"):
        vals = words.view(ml_dtypes.float8_e4m3fn if fmt == "e4m3" else ml_dtypes.float8_e5m2).astype(np.float64)
    else:
        nib = np.empty((g, 128, n, 4), np.uint8)
        nib[..., 0::2] = words & 0xF
        nib[..., 1::2] = words >> 4
        vals = E2M1[nib]
    vals = vals * np.repeat(np.exp2(scales.astype(np.float64) - 127.0), 8, axis=1)[..., None]
    return vals.transpose(0, 1, 3, 2).reshape(g * 512, n)


def bf(x):
    return np.asarray(x, np.float32).astype(ml_dtypes.bfloat16)


def planes(Y):
    r, m = Y.shape
    b = f64(bf(Y)).reshape(r // 32, 32, m)
    amax = np.abs(b).max(1)
    byte = np.clip(np.where(amax > 0, np.frexp(amax)[1] - 1 + 127 - 7, 1), 1, 254)
    codes = (b * np.exp2(127.0 - byte)[:, None, :]).reshape(r, m).astype(np.float32).astype(ml_dtypes.float8_e4m3fn).view(np.uint8)
    words = codes.reshape(r // 512, 128, 4, m).transpose(0, 1, 3, 2)
    return np.ascontiguousarray(words), np.ascontiguousarray(byte.astype(np.uint8).reshape(r // 512, 16, m))


K, T, J, R, O, N, E = 512, 2048, 256, 512, 128, 512, 1024


def setup_inputs():
    n = np.random.standard_normal
    idx = np.random.permutation(T)[:J]
    idx2 = np.random.permutation(T)[:J]
    idx3 = np.random.permutation(J)[:O]
    idx4 = np.random.permutation(J)[:O]
    idx5 = np.random.permutation(E)[:O]
    fk = mx_kscale(K)
    fr = mx_kscale(R)
    xtp = pack_weight(n((K, T)) / fk[:, None], "e5m2")
    wp = pack_weight(n((K, R)) * 1 / np.sqrt(K) * fk[:, None] * fr, "e2m1")
    wbp = pack_weight(n((R, N)) * 1 / np.sqrt(R) / fr[:, None], "e2m1")
    return {
        "xt_words": xtp[0],
        "xt_scales": xtp[1],
        "w_words": wp[0],
        "w_scales": wp[1],
        "wb_words": wbp[0],
        "wb_scales": wbp[1],
        "tz": (n((N, E))).astype(np.float32),
        "offs": striped(idx),
        "offs2": striped(idx2),
        "offs3": striped(idx3),
        "offs4": striped(idx4),
        "offs5": striped(idx5),
    }


def reference(xt_words, xt_scales, w_words, w_scales, wb_words, wb_scales, tz, offs, offs2, offs3, offs4, offs5):
    idx = unstriped(offs)
    idx2 = unstriped(offs2)
    idx3 = unstriped(offs3)
    idx4 = unstriped(offs4)
    idx5 = unstriped(offs5)
    xtu = unpack_weight(xt_words, xt_scales, "e5m2")
    wu = unpack_weight(w_words, w_scales, "e2m1")
    wbu = unpack_weight(wb_words, wb_scales, "e2m1")
    xtidxg = xtu[:, idx]
    a = wu.T @ xtidxg
    xtidx2g = xtu[:, idx2]
    b = wu.T @ xtidx2g
    hid = np.abs(a[:, idx3] - b[:, idx4])
    hidq = mxq(hid, 0, "e4m3")
    p = wbu.T @ hidq
    y = p + f64(tz)[:, idx5]
    words, scales = planes(y)
    return y, words, scales

@@ -1,0 +1,200 @@
+from contextlib import ExitStack
+
+import concourse.mybir as mybir
+
+K, T, J, R, O, N, E = 512, 2048, 256, 512, 128, 512, 1024
+FLOPS = 2 * K * R * J * 2 + 2 * R * N * O
+
+F32 = mybir.dt.float32
+BF16 = mybir.dt.bfloat16
+I32 = mybir.dt.int32
+U32 = mybir.dt.uint32
+U16 = mybir.dt.uint16
+U8 = mybir.dt.uint8
+E4M3 = mybir.dt.float8_e4m3fn_x4
+E5M2 = mybir.dt.float8_e5m2_x4
+E2M1 = mybir.dt.float4_e2m1fn_x4
+ACT = mybir.ActivationFunctionType
+ALU = mybir.AluOpType
+
+P = 128
+PACK = 4
+QUADS = 4
+ABS_SPLIT = 72
+
+
+def load_scale_rows(queues, plane, rows):
+    for q in range(QUADS):
+        queues[q].dma_start(
+            out=plane[32 * q : 32 * q + 4, :].bitcast(I32),
+            in_=rows[0, 4 * q : 4 * q + 4, :].bitcast(I32),
+        )
+
+
+def dealt(view):
+    return view.rearrange("p (m t) -> p t m", t=PACK)
+
+
+def slices(view):
+    return view.rearrange("p (t m) -> p t m", t=PACK)
+
+
+def tile_list_tied_looked_one_tabled_pl_kernel(
+    tc, xt_words, xt_scales, w_words, w_scales, wb_words, wb_scales, tz,
+    offs, offs2, offs3, offs4, offs5, out_0, out_1, out_2,
+):
+    nc = tc.nc
+    with ExitStack() as ctx:
+        lists = ctx.enter_context(tc.tile_pool(name="lists", bufs=1))
+        keep = ctx.enter_context(tc.tile_pool(name="keep", bufs=1))
+        psum = ctx.enter_context(tc.psum_pool(name="psum", bufs=1))
+
+        tok_a = lists.tile([P, J // 16], U16, name="tok_a")
+        tok_b = lists.tile([P, J // 16], U16, name="tok_b")
+        slot_a = lists.tile([P, O // 16], U16, name="slot_a")
+        slot_b = lists.tile([P, O // 16], U16, name="slot_b")
+        entry = lists.tile([P, O // 16], U16, name="entry")
+
+        x_words = keep.tile([P, T], U32, name="x_words", align_bytes=64)
+        x_plane = keep.tile([P, T], U8, name="x_plane", align_bytes=64)
+        w_raw = keep.tile([P, 2 * R], U8, name="w_raw", align_bytes=64)
+        wb_raw = keep.tile([P, 2 * N], U8, name="wb_raw", align_bytes=64)
+        raw_plane = keep.tile([P, R], U8, name="raw_plane", align_bytes=64)
+        tz_rows = [keep.tile([P, 2, E], F32, name=f"tz_rows{h}") for h in range(2)]
+
+        nc.vector.memset(x_plane[:].bitcast(I32), 0)
+        nc.vector.memset(raw_plane[:].bitcast(I32), 0)
+
+        nc.sync.dma_start(tok_a[:], offs)
+        nc.sync.dma_start(tok_b[:], offs2)
+        nc.sync.dma_start(out=w_raw[:].bitcast(I32), in_=w_words[0].bitcast(I32))
+        load_scale_rows((nc.sync, nc.scalar, nc.sync, nc.scalar), x_plane, xt_scales)
+        nc.sync.dma_start(
+            out=x_words[:].bitcast(I32),
+            in_=xt_words[0].rearrange("p c r -> p (c r)").bitcast(I32),
+        )
+        load_scale_rows([nc.sync] * QUADS, raw_plane, w_scales)
+        nc.sync.dma_start(out=wb_raw[:].bitcast(I32), in_=wb_words[0].bitcast(I32))
+        nc.sync.dma_start(slot_a[:], offs3)
+        tz_by_partition = tz.rearrange("(p t) e -> p t e", t=PACK)
+        nc.sync.dma_start(out=tz_rows[0][:], in_=tz_by_partition[:, 0:2, :])
+        nc.sync.dma_start(slot_b[:], offs4)
+        nc.sync.dma_start(entry[:], offs5)
+
+        xa_plane = keep.tile([P, J], U8, name="xa_plane", align_bytes=64)
+        xb_plane = keep.tile([P, J], U8, name="xb_plane", align_bytes=64)
+        xa_words = keep.tile([P, J], U32, name="xa_words", align_bytes=64)
+        xb_words = keep.tile([P, J], U32, name="xb_words", align_bytes=64)
+        w_codes = keep.tile([P, 2 * R], U8, name="w_codes", align_bytes=64)
+        w_plane = keep.tile([P, R], U8, name="w_plane", align_bytes=64)
+
+        nc.vector.tensor_copy(slices(w_codes[:].bitcast(U16)), dealt(w_raw[:].bitcast(U16)))
+        nc.vector.tensor_copy(xa_plane[:], x_plane[:].indirect(tok_a[:]))
+        nc.vector.tensor_copy(xb_plane[:], x_plane[:].indirect(tok_b[:]))
+        nc.vector.tensor_copy(xa_words[:], x_words[:].indirect(tok_a[:]))
+        nc.vector.tensor_copy(slices(w_plane[:]), dealt(raw_plane[:]))
+        load_scale_rows([nc.sync] * QUADS, raw_plane, wb_scales)
+        nc.sync.dma_start(out=tz_rows[1][:], in_=tz_by_partition[:, 2:4, :])
+        nc.vector.tensor_copy(xb_words[:], x_words[:].indirect(tok_b[:]))
+        wb_codes = keep.tile([P, 2 * N], U8, name="wb_codes", align_bytes=64)
+        nc.vector.tensor_copy(slices(wb_codes[:].bitcast(U16)), dealt(wb_raw[:].bitcast(U16)))
+
+        def first_product(t, words, plane, bank, name, on_vector):
+            acc = psum.tile([P, J], F32, name=name + "_acc", tag=bank)
+            nc.tensor.matmul_mx(
+                out=acc[:],
+                lhsT=w_codes[:, 2 * P * t : 2 * P * (t + 1)].bitcast(E2M1),
+                lhsT_scale=w_plane[:, P * t : P * (t + 1)],
+                rhs=words[:].bitcast(E5M2),
+                rhs_scale=plane[:],
+                start=True,
+                stop=True,
+            )
+            whole = keep.tile([P, J], F32, name=name, tag=name, align_bytes=64)
+            if on_vector:
+                nc.vector.tensor_copy(whole[:], acc[:])
+            else:
+                nc.scalar.activation(whole[:], acc[:], ACT.Copy)
+            return whole
+
+        picked_a = keep.tile([P, PACK, O], F32, name="picked_a", tag="picked_a", align_bytes=64)
+        diff = keep.tile([P, PACK, O], F32, name="diff", tag="diff")
+
+        def product_a(t):
+            return first_product(t, xa_words, xa_plane, f"bank{t}", f"a{t}", t == 1)
+
+        def product_b(t):
+            return first_product(t, xb_words, xb_plane, f"bank{PACK + t}", f"b{t}", False)
+
+        def pick_a(t, a_rows):
+            if t < PACK - 1:
+                nc.vector.tensor_copy(picked_a[:, t, :], a_rows[:].indirect(slot_a[:]))
+            else:
+                nc.scalar.activation(picked_a[:, t, :], a_rows[:].indirect(slot_a[:]), ACT.Copy)
+
+        def subtract(t, b_rows):
+            nc.vector.tensor_tensor(diff[:, t, :], b_rows[:].indirect(slot_b[:]), picked_a[:, t, :], ALU.subtract)
+
+        early = [product_a(t) for t in range(2)]
+        for t in range(2):
+            pick_a(t, early[t])
+        for t in range(2):
+            subtract(t, product_b(t))
+        for t in range(2, PACK):
+            a_rows = product_a(t)
+            b_rows = product_b(t)
+            pick_a(t, a_rows)
+            subtract(t, b_rows)
+
+        hid = keep.tile([P, O, PACK], BF16, name="hid", align_bytes=64)
+        by_place = diff[:].rearrange("p t o -> p o t")
+        nc.scalar.activation(hid[:, :ABS_SPLIT, :], by_place[:, :ABS_SPLIT, :], ACT.Abs)
+        nc.vector.scalar_tensor_tensor(
+            hid[:, ABS_SPLIT:, :], by_place[:, ABS_SPLIT:, :], -1.0, by_place[:, ABS_SPLIT:, :], ALU.mult, ALU.max
+        )
+        wb_plane = keep.tile([P, N], U8, name="wb_plane", tag="picked_a", align_bytes=64)
+        nc.vector.tensor_copy(slices(wb_plane[:]), dealt(raw_plane[:]))
+        picked_z = keep.tile([P, PACK, O], F32, name="picked_z", tag="diff")
+        hid_codes = keep.tile([P, O], U32, name="hid_codes", align_bytes=64)
+        hid_plane = keep.tile([P, O], U8, name="hid_plane", align_bytes=64)
+        nc.vector.quantize_mx(
+            out=hid_codes[:].bitcast(E4M3), scales=hid_plane[:], in_=hid[:].rearrange("p o t -> p (o t)")
+        )
+        for t in range(PACK):
+            window = tz_rows[t // 2][:, t % 2, :].indirect(entry[:])
+            if t == 1:
+                nc.vector.tensor_copy(picked_z[:, t, :], window)
+            else:
+                nc.scalar.activation(picked_z[:, t, :], window, ACT.Copy)
+
+        y = keep.tile([P, PACK, O], F32, name="y")
+        for t in range(PACK):
+            acc = psum.tile([P, O], F32, name=f"p{t}_acc", tag=f"bank{t}")
+            nc.tensor.matmul_mx(
+                out=acc[:],
+                lhsT=wb_codes[:, 2 * P * t : 2 * P * (t + 1)].bitcast(E2M1),
+                lhsT_scale=wb_plane[:, P * t : P * (t + 1)],
+                rhs=hid_codes[:].bitcast(E4M3),
+                rhs_scale=hid_plane[:],
+                start=True,
+                stop=True,
+            )
+            nc.vector.tensor_tensor(y[:, t, :], acc[:], picked_z[:, t, :], ALU.add)
+        nc.sync.dma_start(out=out_0.rearrange("(p t) o -> p t o", t=PACK), in_=y[:])
+
+        y_rounded = keep.tile([P, O, PACK], BF16, name="y_rounded", align_bytes=64)
+        nc.vector.tensor_copy(y_rounded[:], y[:].rearrange("p t o -> p o t"))
+        y_codes = keep.tile([P, O], U32, name="y_codes", align_bytes=64)
+        y_plane = keep.tile([P, O], U8, name="y_plane", align_bytes=64)
+        nc.vector.quantize_mx(
+            out=y_codes[:].bitcast(E4M3), scales=y_plane[:], in_=y_rounded[:].rearrange("p o t -> p (o t)")
+        )
+        nc.scalar.dma_start(
+            out=out_1[0].rearrange("p c r -> p (c r)").bitcast(I32), in_=y_codes[:].bitcast(I32)
+        )
+        for q in range(QUADS):
+            queue = nc.sync if q < 2 else nc.scalar
+            queue.dma_start(
+                out=out_2[0, 4 * q : 4 * q + 4, :].bitcast(I32),
+                in_=y_plane[32 * q : 32 * q + 4, :].bitcast(I32),
+            )

@@ -20,7 +20,7 @@ ALU = mybir.AluOpType
 P = 128
 PACK = 4
 QUADS = 4
-ABS_SPLIT = 72
+ABS_SPLIT = 64
 
 
 def load_scale_rows(queues, plane, rows):
@@ -59,32 +59,35 @@ def tile_list_tied_looked_one_tabled_pl_kernel(
         x_plane = keep.tile([P, T], U8, name="x_plane", align_bytes=64)
         w_raw = keep.tile([P, 2 * R], U8, name="w_raw", align_bytes=64)
         wb_raw = keep.tile([P, 2 * N], U8, name="wb_raw", align_bytes=64)
-        raw_plane = keep.tile([P, R], U8, name="raw_plane", align_bytes=64)
+        w_plane_raw = keep.tile([P, R], U8, name="w_plane_raw", tag="w_plane_raw", align_bytes=64)
+        wb_plane_raw = keep.tile([P, N], U8, name="wb_plane_raw", align_bytes=64)
         tz_rows = [keep.tile([P, 2, E], F32, name=f"tz_rows{h}") for h in range(2)]
 
         nc.vector.memset(x_plane[:].bitcast(I32), 0)
-        nc.vector.memset(raw_plane[:].bitcast(I32), 0)
+        nc.vector.memset(w_plane_raw[:].bitcast(I32), 0)
+        nc.vector.memset(wb_plane_raw[:].bitcast(I32), 0)
 
         nc.sync.dma_start(tok_a[:], offs)
         nc.sync.dma_start(tok_b[:], offs2)
-        nc.sync.dma_start(out=w_raw[:].bitcast(I32), in_=w_words[0].bitcast(I32))
+        nc.scalar.dma_start(out=w_raw[:].bitcast(I32), in_=w_words[0].bitcast(I32))
         load_scale_rows((nc.sync, nc.scalar, nc.sync, nc.scalar), x_plane, xt_scales)
         nc.sync.dma_start(
             out=x_words[:].bitcast(I32),
             in_=xt_words[0].rearrange("p c r -> p (c r)").bitcast(I32),
         )
-        load_scale_rows([nc.sync] * QUADS, raw_plane, w_scales)
+        load_scale_rows([nc.sync] * QUADS, w_plane_raw, w_scales)
         nc.sync.dma_start(out=wb_raw[:].bitcast(I32), in_=wb_words[0].bitcast(I32))
         nc.sync.dma_start(slot_a[:], offs3)
         tz_by_partition = tz.rearrange("(p t) e -> p t e", t=PACK)
         nc.sync.dma_start(out=tz_rows[0][:], in_=tz_by_partition[:, 0:2, :])
         nc.sync.dma_start(slot_b[:], offs4)
         nc.sync.dma_start(entry[:], offs5)
+        load_scale_rows([nc.sync] * QUADS, wb_plane_raw, wb_scales)
+        nc.sync.dma_start(out=tz_rows[1][:], in_=tz_by_partition[:, 2:4, :])
 
         xa_plane = keep.tile([P, J], U8, name="xa_plane", align_bytes=64)
         xb_plane = keep.tile([P, J], U8, name="xb_plane", align_bytes=64)
         xa_words = keep.tile([P, J], U32, name="xa_words", align_bytes=64)
-        xb_words = keep.tile([P, J], U32, name="xb_words", align_bytes=64)
         w_codes = keep.tile([P, 2 * R], U8, name="w_codes", align_bytes=64)
         w_plane = keep.tile([P, R], U8, name="w_plane", align_bytes=64)
 
@@ -92,9 +95,9 @@ def tile_list_tied_looked_one_tabled_pl_kernel(
         nc.vector.tensor_copy(xa_plane[:], x_plane[:].indirect(tok_a[:]))
         nc.vector.tensor_copy(xb_plane[:], x_plane[:].indirect(tok_b[:]))
         nc.vector.tensor_copy(xa_words[:], x_words[:].indirect(tok_a[:]))
-        nc.vector.tensor_copy(slices(w_plane[:]), dealt(raw_plane[:]))
-        load_scale_rows([nc.sync] * QUADS, raw_plane, wb_scales)
-        nc.sync.dma_start(out=tz_rows[1][:], in_=tz_by_partition[:, 2:4, :])
+        for half in (slice(0, 2), slice(2, PACK)):
+            nc.vector.tensor_copy(slices(w_plane[:])[:, half, :], dealt(w_plane_raw[:])[:, half, :])
+        xb_words = keep.tile([P, J], U32, name="xb_words", tag="w_plane_raw", align_bytes=64)
         nc.vector.tensor_copy(xb_words[:], x_words[:].indirect(tok_b[:]))
         wb_codes = keep.tile([P, 2 * N], U8, name="wb_codes", align_bytes=64)
         nc.vector.tensor_copy(slices(wb_codes[:].bitcast(U16)), dealt(wb_raw[:].bitcast(U16)))
@@ -117,7 +120,7 @@ def tile_list_tied_looked_one_tabled_pl_kernel(
                 nc.scalar.activation(whole[:], acc[:], ACT.Copy)
             return whole
 
-        picked_a = keep.tile([P, PACK, O], F32, name="picked_a", tag="picked_a", align_bytes=64)
+        picked_a = keep.tile([P, PACK, O], F32, name="picked_a")
         diff = keep.tile([P, PACK, O], F32, name="diff", tag="diff")
 
         def product_a(t):
@@ -135,25 +138,24 @@ def tile_list_tied_looked_one_tabled_pl_kernel(
         def subtract(t, b_rows):
             nc.vector.tensor_tensor(diff[:, t, :], b_rows[:].indirect(slot_b[:]), picked_a[:, t, :], ALU.subtract)
 
-        early = [product_a(t) for t in range(2)]
-        for t in range(2):
-            pick_a(t, early[t])
+        for t in range(PACK - 1):
+            pick_a(t, product_a(t))
         for t in range(2):
             subtract(t, product_b(t))
-        for t in range(2, PACK):
-            a_rows = product_a(t)
-            b_rows = product_b(t)
-            pick_a(t, a_rows)
-            subtract(t, b_rows)
+        a_last = product_a(PACK - 1)
+        subtract(2, product_b(2))
+        b_last = product_b(PACK - 1)
+        pick_a(PACK - 1, a_last)
+        subtract(PACK - 1, b_last)
 
+        wb_plane = keep.tile([P, N], U8, name="wb_plane", tag=f"a{PACK - 1}", align_bytes=64)
+        nc.vector.tensor_copy(slices(wb_plane[:]), dealt(wb_plane_raw[:]))
         hid = keep.tile([P, O, PACK], BF16, name="hid", align_bytes=64)
         by_place = diff[:].rearrange("p t o -> p o t")
         nc.scalar.activation(hid[:, :ABS_SPLIT, :], by_place[:, :ABS_SPLIT, :], ACT.Abs)
         nc.vector.scalar_tensor_tensor(
             hid[:, ABS_SPLIT:, :], by_place[:, ABS_SPLIT:, :], -1.0, by_place[:, ABS_SPLIT:, :], ALU.mult, ALU.max
         )
-        wb_plane = keep.tile([P, N], U8, name="wb_plane", tag="picked_a", align_bytes=64)
-        nc.vector.tensor_copy(slices(wb_plane[:]), dealt(raw_plane[:]))
         picked_z = keep.tile([P, PACK, O], F32, name="picked_z", tag="diff")
         hid_codes = keep.tile([P, O], U32, name="hid_codes", align_bytes=64)
         hid_plane = keep.tile([P, O], U8, name="hid_plane", align_bytes=64)
@@ -161,11 +163,7 @@ def tile_list_tied_looked_one_tabled_pl_kernel(
             out=hid_codes[:].bitcast(E4M3), scales=hid_plane[:], in_=hid[:].rearrange("p o t -> p (o t)")
         )
         for t in range(PACK):
-            window = tz_rows[t // 2][:, t % 2, :].indirect(entry[:])
-            if t == 1:
-                nc.vector.tensor_copy(picked_z[:, t, :], window)
-            else:
-                nc.scalar.activation(picked_z[:, t, :], window, ACT.Copy)
+            nc.scalar.activation(picked_z[:, t, :], tz_rows[t // 2][:, t % 2, :].indirect(entry[:]), ACT.Copy)
 
         y = keep.tile([P, PACK, O], F32, name="y")
         for t in range(PACK):

@@ -21,6 +21,7 @@ P = 128
 PACK = 4
 QUADS = 4
 ABS_SPLIT = 64
+HALVES = (slice(0, O // 2), slice(O // 2, O))
 
 
 def load_scale_rows(queues, plane, rows):
@@ -37,6 +38,14 @@ def dealt(view):
 
 def slices(view):
     return view.rearrange("p (t m) -> p t m", t=PACK)
+
+
+def quantize(nc, codes, plane, rounded, places):
+    nc.vector.quantize_mx(
+        out=codes[:, places].bitcast(E4M3),
+        scales=plane[:, places],
+        in_=rounded[:, places, :].rearrange("p o t -> p (o t)"),
+    )
 
 
 def tile_list_tied_looked_one_tabled_pl_kernel(
@@ -150,20 +159,23 @@ def tile_list_tied_looked_one_tabled_pl_kernel(
 
         wb_plane = keep.tile([P, N], U8, name="wb_plane", tag=f"a{PACK - 1}", align_bytes=64)
         nc.vector.tensor_copy(slices(wb_plane[:]), dealt(wb_plane_raw[:]))
-        hid = keep.tile([P, O, PACK], BF16, name="hid", align_bytes=64)
+        hid = keep.tile([P, O, PACK], BF16, name="hid", tag="hid", align_bytes=64)
         by_place = diff[:].rearrange("p t o -> p o t")
         nc.scalar.activation(hid[:, :ABS_SPLIT, :], by_place[:, :ABS_SPLIT, :], ACT.Abs)
         nc.vector.scalar_tensor_tensor(
             hid[:, ABS_SPLIT:, :], by_place[:, ABS_SPLIT:, :], -1.0, by_place[:, ABS_SPLIT:, :], ALU.mult, ALU.max
         )
-        picked_z = keep.tile([P, PACK, O], F32, name="picked_z", tag="diff")
         hid_codes = keep.tile([P, O], U32, name="hid_codes", align_bytes=64)
         hid_plane = keep.tile([P, O], U8, name="hid_plane", align_bytes=64)
-        nc.vector.quantize_mx(
-            out=hid_codes[:].bitcast(E4M3), scales=hid_plane[:], in_=hid[:].rearrange("p o t -> p (o t)")
-        )
-        for t in range(PACK):
-            nc.scalar.activation(picked_z[:, t, :], tz_rows[t // 2][:, t % 2, :].indirect(entry[:]), ACT.Copy)
+        for half in (HALVES[1], HALVES[0]):
+            quantize(nc, hid_codes, hid_plane, hid, half)
+        picked_z = [
+            keep.tile([P, 2, O], F32, name="picked_z0", tag="diff"),
+            keep.tile([P, 2, O], F32, name="picked_z1", tag="hid", align_bytes=64),
+        ]
+        for u in range(2):
+            nc.scalar.activation(picked_z[0][:, u, :], tz_rows[0][:, u, :].indirect(entry[:]), ACT.Copy)
+            nc.vector.tensor_copy(picked_z[1][:, u, :], tz_rows[1][:, u, :].indirect(entry[:]))
 
         y = keep.tile([P, PACK, O], F32, name="y")
         for t in range(PACK):
@@ -177,16 +189,17 @@ def tile_list_tied_looked_one_tabled_pl_kernel(
                 start=True,
                 stop=True,
             )
-            nc.vector.tensor_tensor(y[:, t, :], acc[:], picked_z[:, t, :], ALU.add)
+            for places in HALVES if t == PACK - 1 else (slice(0, O),):
+                nc.vector.tensor_tensor(y[:, t, places], acc[:, places], picked_z[t // 2][:, t % 2, places], ALU.add)
         nc.sync.dma_start(out=out_0.rearrange("(p t) o -> p t o", t=PACK), in_=y[:])
 
         y_rounded = keep.tile([P, O, PACK], BF16, name="y_rounded", align_bytes=64)
-        nc.vector.tensor_copy(y_rounded[:], y[:].rearrange("p t o -> p o t"))
+        for half in HALVES:
+            nc.vector.tensor_copy(y_rounded[:, half, :], y[:].rearrange("p t o -> p o t")[:, half, :])
         y_codes = keep.tile([P, O], U32, name="y_codes", align_bytes=64)
         y_plane = keep.tile([P, O], U8, name="y_plane", align_bytes=64)
-        nc.vector.quantize_mx(
-            out=y_codes[:].bitcast(E4M3), scales=y_plane[:], in_=y_rounded[:].rearrange("p o t -> p (o t)")
-        )
+        for half in HALVES:
+            quantize(nc, y_codes, y_plane, y_rounded, half)
         nc.scalar.dma_start(
             out=out_1[0].rearrange("p c r -> p (c r)").bitcast(I32), in_=y_codes[:].bitcast(I32)
         )

@@ -20,7 +20,6 @@ ALU = mybir.AluOpType
 P = 128
 PACK = 4
 QUADS = 4
-ABS_SPLIT = 64
 HALVES = (slice(0, O // 2), slice(O // 2, O))
 
 
@@ -38,6 +37,10 @@ def dealt(view):
 
 def slices(view):
     return view.rearrange("p (t m) -> p t m", t=PACK)
+
+
+def entries(offsets, places):
+    return offsets[:, places.start // 16 : places.stop // 16]
 
 
 def quantize(nc, codes, plane, rounded, places):
@@ -69,7 +72,7 @@ def tile_list_tied_looked_one_tabled_pl_kernel(
         w_raw = keep.tile([P, 2 * R], U8, name="w_raw", align_bytes=64)
         wb_raw = keep.tile([P, 2 * N], U8, name="wb_raw", align_bytes=64)
         w_plane_raw = keep.tile([P, R], U8, name="w_plane_raw", tag="w_plane_raw", align_bytes=64)
-        wb_plane_raw = keep.tile([P, N], U8, name="wb_plane_raw", align_bytes=64)
+        wb_plane_raw = keep.tile([P, N], U8, name="wb_plane_raw", tag="wb_plane_raw", align_bytes=64)
         tz_rows = [keep.tile([P, 2, E], F32, name=f"tz_rows{h}") for h in range(2)]
 
         nc.vector.memset(x_plane[:].bitcast(I32), 0)
@@ -111,7 +114,7 @@ def tile_list_tied_looked_one_tabled_pl_kernel(
         wb_codes = keep.tile([P, 2 * N], U8, name="wb_codes", align_bytes=64)
         nc.vector.tensor_copy(slices(wb_codes[:].bitcast(U16)), dealt(wb_raw[:].bitcast(U16)))
 
-        def first_product(t, words, plane, bank, name, on_vector):
+        def first_product(t, words, plane, bank, name):
             acc = psum.tile([P, J], F32, name=name + "_acc", tag=bank)
             nc.tensor.matmul_mx(
                 out=acc[:],
@@ -123,59 +126,54 @@ def tile_list_tied_looked_one_tabled_pl_kernel(
                 stop=True,
             )
             whole = keep.tile([P, J], F32, name=name, tag=name, align_bytes=64)
-            if on_vector:
-                nc.vector.tensor_copy(whole[:], acc[:])
-            else:
-                nc.scalar.activation(whole[:], acc[:], ACT.Copy)
+            nc.scalar.activation(whole[:], acc[:], ACT.Copy)
             return whole
 
         picked_a = keep.tile([P, PACK, O], F32, name="picked_a")
         diff = keep.tile([P, PACK, O], F32, name="diff", tag="diff")
 
         def product_a(t):
-            return first_product(t, xa_words, xa_plane, f"bank{t}", f"a{t}", t == 1)
+            return first_product(t, xa_words, xa_plane, f"bank{t}", f"a{t}")
 
         def product_b(t):
-            return first_product(t, xb_words, xb_plane, f"bank{PACK + t}", f"b{t}", False)
+            return first_product(t, xb_words, xb_plane, f"bank{PACK + t}", f"b{t}")
 
-        def pick_a(t, a_rows):
-            if t < PACK - 1:
-                nc.vector.tensor_copy(picked_a[:, t, :], a_rows[:].indirect(slot_a[:]))
-            else:
-                nc.scalar.activation(picked_a[:, t, :], a_rows[:].indirect(slot_a[:]), ACT.Copy)
+        def subtract(t, b_rows, places):
+            nc.vector.tensor_tensor(
+                diff[:, t, places], b_rows[:].indirect(entries(slot_b, places)), picked_a[:, t, places], ALU.subtract
+            )
 
-        def subtract(t, b_rows):
-            nc.vector.tensor_tensor(diff[:, t, :], b_rows[:].indirect(slot_b[:]), picked_a[:, t, :], ALU.subtract)
+        last = PACK - 1
+        for t in range(last):
+            nc.vector.tensor_copy(picked_a[:, t, :], product_a(t)[:].indirect(slot_a[:]))
+        for t in range(last):
+            subtract(t, product_b(t), slice(0, O))
+        wb_plane = keep.tile([P, N], U8, name="wb_plane", align_bytes=64)
+        a_last = product_a(last)
+        b_last = product_b(last)
+        for half in HALVES:
+            nc.scalar.activation(picked_a[:, last, half], a_last[:].indirect(entries(slot_a, half)), ACT.Copy)
+            subtract(last, b_last, half)
 
-        for t in range(PACK - 1):
-            pick_a(t, product_a(t))
-        for t in range(2):
-            subtract(t, product_b(t))
-        a_last = product_a(PACK - 1)
-        subtract(2, product_b(2))
-        b_last = product_b(PACK - 1)
-        pick_a(PACK - 1, a_last)
-        subtract(PACK - 1, b_last)
-
-        wb_plane = keep.tile([P, N], U8, name="wb_plane", tag=f"a{PACK - 1}", align_bytes=64)
-        nc.vector.tensor_copy(slices(wb_plane[:]), dealt(wb_plane_raw[:]))
         hid = keep.tile([P, O, PACK], BF16, name="hid", tag="hid", align_bytes=64)
         by_place = diff[:].rearrange("p t o -> p o t")
-        nc.scalar.activation(hid[:, :ABS_SPLIT, :], by_place[:, :ABS_SPLIT, :], ACT.Abs)
+        low, high = HALVES
         nc.vector.scalar_tensor_tensor(
-            hid[:, ABS_SPLIT:, :], by_place[:, ABS_SPLIT:, :], -1.0, by_place[:, ABS_SPLIT:, :], ALU.mult, ALU.max
+            hid[:, low, :], by_place[:, low, :], -1.0, by_place[:, low, :], ALU.mult, ALU.max
         )
-        hid_codes = keep.tile([P, O], U32, name="hid_codes", align_bytes=64)
+        nc.scalar.activation(hid[:, high, :], by_place[:, high, :], ACT.Abs)
+        nc.vector.tensor_copy(slices(wb_plane[:]), dealt(wb_plane_raw[:]))
+        hid_codes = keep.tile([P, O], U32, name="hid_codes", tag="wb_plane_raw", align_bytes=64)
         hid_plane = keep.tile([P, O], U8, name="hid_plane", align_bytes=64)
-        for half in (HALVES[1], HALVES[0]):
+        for half in HALVES:
             quantize(nc, hid_codes, hid_plane, hid, half)
         picked_z = [
-            keep.tile([P, 2, O], F32, name="picked_z0", tag="diff"),
-            keep.tile([P, 2, O], F32, name="picked_z1", tag="hid", align_bytes=64),
+            keep.tile([P, 2, O], F32, name="picked_z0", tag="hid", align_bytes=64),
+            keep.tile([P, 2, O], F32, name="picked_z1", tag="diff"),
         ]
         for u in range(2):
-            nc.scalar.activation(picked_z[0][:, u, :], tz_rows[0][:, u, :].indirect(entry[:]), ACT.Copy)
-            nc.vector.tensor_copy(picked_z[1][:, u, :], tz_rows[1][:, u, :].indirect(entry[:]))
+            nc.vector.tensor_copy(picked_z[0][:, u, :], tz_rows[0][:, u, :].indirect(entry[:]))
+            nc.scalar.activation(picked_z[1][:, u, :], tz_rows[1][:, u, :].indirect(entry[:]), ACT.Copy)
 
         y = keep.tile([P, PACK, O], F32, name="y")
         for t in range(PACK):

@@ -20,27 +20,40 @@ ALU = mybir.AluOpType
 P = 128
 PACK = 4
 QUADS = 4
+QUAD_ROWS = P // QUADS
+GROUP = 16
+RUN = 4
+ALIGN = 64
 HALVES = (slice(0, O // 2), slice(O // 2, O))
+SLICE_PAIRS = (slice(0, 2), slice(2, PACK))
 
 
-def load_scale_rows(queues, plane, rows):
-    for q in range(QUADS):
-        queues[q].dma_start(
-            out=plane[32 * q : 32 * q + 4, :].bitcast(I32),
-            in_=rows[0, 4 * q : 4 * q + 4, :].bitcast(I32),
+def load_plane(queues, plane, rows):
+    for quad in range(QUADS):
+        queues[quad].dma_start(
+            out=plane[QUAD_ROWS * quad : QUAD_ROWS * quad + PACK, :].bitcast(I32),
+            in_=rows[0, PACK * quad : PACK * quad + PACK, :].bitcast(I32),
         )
 
 
-def dealt(view):
-    return view.rearrange("p (m t) -> p t m", t=PACK)
+def dealt(columns):
+    return columns.rearrange("p (m t) -> p t m", t=PACK)
 
 
-def slices(view):
-    return view.rearrange("p (t m) -> p t m", t=PACK)
+def slices(places):
+    return places.rearrange("p (t m) -> p t m", t=PACK)
 
 
 def entries(offsets, places):
-    return offsets[:, places.start // 16 : places.stop // 16]
+    return offsets[:, places.start // GROUP : places.stop // GROUP]
+
+
+def in_runs(by_slice, places):
+    return by_slice[:, :, places].rearrange("p t (c i) -> p c t i", i=RUN)
+
+
+def woven(by_place, places):
+    return by_place[:, places, :].rearrange("p (c i) t -> p c t i", i=RUN)
 
 
 def quantize(nc, codes, plane, rounded, places):
@@ -48,6 +61,18 @@ def quantize(nc, codes, plane, rounded, places):
         out=codes[:, places].bitcast(E4M3),
         scales=plane[:, places],
         in_=rounded[:, places, :].rearrange("p o t -> p (o t)"),
+    )
+
+
+def multiply(nc, acc, weight_codes, weight_plane, t, moving, moving_plane):
+    nc.tensor.matmul_mx(
+        out=acc[:],
+        lhsT=weight_codes[:, 2 * P * t : 2 * P * (t + 1)].bitcast(E2M1),
+        lhsT_scale=weight_plane[:, P * t : P * (t + 1)],
+        rhs=moving,
+        rhs_scale=moving_plane[:],
+        start=True,
+        stop=True,
     )
 
 
@@ -61,19 +86,19 @@ def tile_list_tied_looked_one_tabled_pl_kernel(
         keep = ctx.enter_context(tc.tile_pool(name="keep", bufs=1))
         psum = ctx.enter_context(tc.psum_pool(name="psum", bufs=1))
 
-        tok_a = lists.tile([P, J // 16], U16, name="tok_a")
-        tok_b = lists.tile([P, J // 16], U16, name="tok_b")
-        slot_a = lists.tile([P, O // 16], U16, name="slot_a")
-        slot_b = lists.tile([P, O // 16], U16, name="slot_b")
-        entry = lists.tile([P, O // 16], U16, name="entry")
+        tok_a = lists.tile([P, J // GROUP], U16, name="tok_a")
+        tok_b = lists.tile([P, J // GROUP], U16, name="tok_b")
+        slot_a = lists.tile([P, O // GROUP], U16, name="slot_a")
+        slot_b = lists.tile([P, O // GROUP], U16, name="slot_b")
+        entry = lists.tile([P, O // GROUP], U16, name="entry")
 
-        x_words = keep.tile([P, T], U32, name="x_words", align_bytes=64)
-        x_plane = keep.tile([P, T], U8, name="x_plane", align_bytes=64)
-        w_raw = keep.tile([P, 2 * R], U8, name="w_raw", align_bytes=64)
-        wb_raw = keep.tile([P, 2 * N], U8, name="wb_raw", align_bytes=64)
-        w_plane_raw = keep.tile([P, R], U8, name="w_plane_raw", tag="w_plane_raw", align_bytes=64)
-        wb_plane_raw = keep.tile([P, N], U8, name="wb_plane_raw", tag="wb_plane_raw", align_bytes=64)
-        tz_rows = [keep.tile([P, 2, E], F32, name=f"tz_rows{h}") for h in range(2)]
+        x_words = keep.tile([P, T], U32, name="x_words", align_bytes=ALIGN)
+        x_plane = keep.tile([P, T], U8, name="x_plane", align_bytes=ALIGN)
+        w_raw = keep.tile([P, 2 * R], U8, name="w_raw", align_bytes=ALIGN)
+        wb_raw = keep.tile([P, 2 * N], U8, name="wb_raw", align_bytes=ALIGN)
+        w_plane_raw = keep.tile([P, R], U8, name="w_plane_raw", tag="w_plane_raw", align_bytes=ALIGN)
+        wb_plane_raw = keep.tile([P, N], U8, name="wb_plane_raw", tag="wb_plane_raw", align_bytes=ALIGN)
+        tz_rows = [keep.tile([P, 2, E], F32, name=f"tz_rows{pair}") for pair in range(2)]
 
         nc.vector.memset(x_plane[:].bitcast(I32), 0)
         nc.vector.memset(w_plane_raw[:].bitcast(I32), 0)
@@ -82,50 +107,42 @@ def tile_list_tied_looked_one_tabled_pl_kernel(
         nc.sync.dma_start(tok_a[:], offs)
         nc.sync.dma_start(tok_b[:], offs2)
         nc.scalar.dma_start(out=w_raw[:].bitcast(I32), in_=w_words[0].bitcast(I32))
-        load_scale_rows((nc.sync, nc.scalar, nc.sync, nc.scalar), x_plane, xt_scales)
+        load_plane((nc.sync, nc.scalar, nc.sync, nc.scalar), x_plane, xt_scales)
         nc.sync.dma_start(
             out=x_words[:].bitcast(I32),
             in_=xt_words[0].rearrange("p c r -> p (c r)").bitcast(I32),
         )
-        load_scale_rows([nc.sync] * QUADS, w_plane_raw, w_scales)
+        load_plane([nc.sync] * QUADS, w_plane_raw, w_scales)
         nc.sync.dma_start(out=wb_raw[:].bitcast(I32), in_=wb_words[0].bitcast(I32))
         nc.sync.dma_start(slot_a[:], offs3)
-        tz_by_partition = tz.rearrange("(p t) e -> p t e", t=PACK)
-        nc.sync.dma_start(out=tz_rows[0][:], in_=tz_by_partition[:, 0:2, :])
+        tz_by_slice = tz.rearrange("(p t) e -> p t e", t=PACK)
+        nc.sync.dma_start(out=tz_rows[0][:], in_=tz_by_slice[:, SLICE_PAIRS[0], :])
         nc.sync.dma_start(slot_b[:], offs4)
         nc.sync.dma_start(entry[:], offs5)
-        load_scale_rows([nc.sync] * QUADS, wb_plane_raw, wb_scales)
-        nc.sync.dma_start(out=tz_rows[1][:], in_=tz_by_partition[:, 2:4, :])
+        load_plane([nc.sync] * QUADS, wb_plane_raw, wb_scales)
+        nc.sync.dma_start(out=tz_rows[1][:], in_=tz_by_slice[:, SLICE_PAIRS[1], :])
 
-        xa_plane = keep.tile([P, J], U8, name="xa_plane", align_bytes=64)
-        xb_plane = keep.tile([P, J], U8, name="xb_plane", align_bytes=64)
-        xa_words = keep.tile([P, J], U32, name="xa_words", align_bytes=64)
-        w_codes = keep.tile([P, 2 * R], U8, name="w_codes", align_bytes=64)
-        w_plane = keep.tile([P, R], U8, name="w_plane", align_bytes=64)
+        xa_plane = keep.tile([P, J], U8, name="xa_plane", align_bytes=ALIGN)
+        xb_plane = keep.tile([P, J], U8, name="xb_plane", align_bytes=ALIGN)
+        xa_words = keep.tile([P, J], U32, name="xa_words", align_bytes=ALIGN)
+        w_codes = keep.tile([P, 2 * R], U8, name="w_codes", align_bytes=ALIGN)
+        w_plane = keep.tile([P, R], U8, name="w_plane", align_bytes=ALIGN)
 
         nc.vector.tensor_copy(slices(w_codes[:].bitcast(U16)), dealt(w_raw[:].bitcast(U16)))
         nc.vector.tensor_copy(xa_plane[:], x_plane[:].indirect(tok_a[:]))
         nc.vector.tensor_copy(xb_plane[:], x_plane[:].indirect(tok_b[:]))
         nc.vector.tensor_copy(xa_words[:], x_words[:].indirect(tok_a[:]))
-        for half in (slice(0, 2), slice(2, PACK)):
-            nc.vector.tensor_copy(slices(w_plane[:])[:, half, :], dealt(w_plane_raw[:])[:, half, :])
-        xb_words = keep.tile([P, J], U32, name="xb_words", tag="w_plane_raw", align_bytes=64)
+        for pair in SLICE_PAIRS:
+            nc.vector.tensor_copy(slices(w_plane[:])[:, pair, :], dealt(w_plane_raw[:])[:, pair, :])
+        xb_words = keep.tile([P, J], U32, name="xb_words", tag="w_plane_raw", align_bytes=ALIGN)
         nc.vector.tensor_copy(xb_words[:], x_words[:].indirect(tok_b[:]))
-        wb_codes = keep.tile([P, 2 * N], U8, name="wb_codes", align_bytes=64)
+        wb_codes = keep.tile([P, 2 * N], U8, name="wb_codes", align_bytes=ALIGN)
         nc.vector.tensor_copy(slices(wb_codes[:].bitcast(U16)), dealt(wb_raw[:].bitcast(U16)))
 
         def first_product(t, words, plane, bank, name):
-            acc = psum.tile([P, J], F32, name=name + "_acc", tag=bank)
-            nc.tensor.matmul_mx(
-                out=acc[:],
-                lhsT=w_codes[:, 2 * P * t : 2 * P * (t + 1)].bitcast(E2M1),
-                lhsT_scale=w_plane[:, P * t : P * (t + 1)],
-                rhs=words[:].bitcast(E5M2),
-                rhs_scale=plane[:],
-                start=True,
-                stop=True,
-            )
-            whole = keep.tile([P, J], F32, name=name, tag=name, align_bytes=64)
+            acc = psum.tile([P, J], F32, name=name + "_acc", tag=f"bank{bank}")
+            multiply(nc, acc, w_codes, w_plane, t, words[:].bitcast(E5M2), plane)
+            whole = keep.tile([P, J], F32, name=name, tag=name, align_bytes=ALIGN)
             nc.scalar.activation(whole[:], acc[:], ACT.Copy)
             return whole
 
@@ -133,10 +150,10 @@ def tile_list_tied_looked_one_tabled_pl_kernel(
         diff = keep.tile([P, PACK, O], F32, name="diff", tag="diff")
 
         def product_a(t):
-            return first_product(t, xa_words, xa_plane, f"bank{t}", f"a{t}")
+            return first_product(t, xa_words, xa_plane, t, f"a{t}")
 
         def product_b(t):
-            return first_product(t, xb_words, xb_plane, f"bank{PACK + t}", f"b{t}")
+            return first_product(t, xb_words, xb_plane, PACK + t, f"b{t}")
 
         def subtract(t, b_rows, places):
             nc.vector.tensor_tensor(
@@ -148,27 +165,24 @@ def tile_list_tied_looked_one_tabled_pl_kernel(
             nc.vector.tensor_copy(picked_a[:, t, :], product_a(t)[:].indirect(slot_a[:]))
         for t in range(last):
             subtract(t, product_b(t), slice(0, O))
-        wb_plane = keep.tile([P, N], U8, name="wb_plane", align_bytes=64)
+        wb_plane = keep.tile([P, N], U8, name="wb_plane", align_bytes=ALIGN)
         a_last = product_a(last)
         b_last = product_b(last)
         for half in HALVES:
             nc.scalar.activation(picked_a[:, last, half], a_last[:].indirect(entries(slot_a, half)), ACT.Copy)
             subtract(last, b_last, half)
 
-        hid = keep.tile([P, O, PACK], BF16, name="hid", tag="hid", align_bytes=64)
-        by_place = diff[:].rearrange("p t o -> p o t")
-        low, high = HALVES
-        nc.vector.scalar_tensor_tensor(
-            hid[:, low, :], by_place[:, low, :], -1.0, by_place[:, low, :], ALU.mult, ALU.max
-        )
-        nc.scalar.activation(hid[:, high, :], by_place[:, high, :], ACT.Abs)
+        hid = keep.tile([P, O, PACK], BF16, name="hid", tag="hid", align_bytes=ALIGN)
+        for half in HALVES:
+            nc.scalar.activation(woven(hid, half), in_runs(diff, half), ACT.Abs)
         nc.vector.tensor_copy(slices(wb_plane[:]), dealt(wb_plane_raw[:]))
-        hid_codes = keep.tile([P, O], U32, name="hid_codes", tag="wb_plane_raw", align_bytes=64)
-        hid_plane = keep.tile([P, O], U8, name="hid_plane", align_bytes=64)
+        hid_codes = keep.tile([P, O], U32, name="hid_codes", tag="wb_plane_raw", align_bytes=ALIGN)
+        hid_plane = keep.tile([P, O], U8, name="hid_plane", align_bytes=ALIGN)
         for half in HALVES:
             quantize(nc, hid_codes, hid_plane, hid, half)
+
         picked_z = [
-            keep.tile([P, 2, O], F32, name="picked_z0", tag="hid", align_bytes=64),
+            keep.tile([P, 2, O], F32, name="picked_z0", tag="hid", align_bytes=ALIGN),
             keep.tile([P, 2, O], F32, name="picked_z1", tag="diff"),
         ]
         for u in range(2):
@@ -178,32 +192,23 @@ def tile_list_tied_looked_one_tabled_pl_kernel(
         y = keep.tile([P, PACK, O], F32, name="y")
         for t in range(PACK):
             acc = psum.tile([P, O], F32, name=f"p{t}_acc", tag=f"bank{t}")
-            nc.tensor.matmul_mx(
-                out=acc[:],
-                lhsT=wb_codes[:, 2 * P * t : 2 * P * (t + 1)].bitcast(E2M1),
-                lhsT_scale=wb_plane[:, P * t : P * (t + 1)],
-                rhs=hid_codes[:].bitcast(E4M3),
-                rhs_scale=hid_plane[:],
-                start=True,
-                stop=True,
-            )
-            for places in HALVES if t == PACK - 1 else (slice(0, O),):
+            multiply(nc, acc, wb_codes, wb_plane, t, hid_codes[:].bitcast(E4M3), hid_plane)
+            for places in HALVES if t == last else (slice(0, O),):
                 nc.vector.tensor_tensor(y[:, t, places], acc[:, places], picked_z[t // 2][:, t % 2, places], ALU.add)
         nc.sync.dma_start(out=out_0.rearrange("(p t) o -> p t o", t=PACK), in_=y[:])
 
-        y_rounded = keep.tile([P, O, PACK], BF16, name="y_rounded", align_bytes=64)
+        y_rounded = keep.tile([P, O, PACK], BF16, name="y_rounded", align_bytes=ALIGN)
         for half in HALVES:
-            nc.vector.tensor_copy(y_rounded[:, half, :], y[:].rearrange("p t o -> p o t")[:, half, :])
-        y_codes = keep.tile([P, O], U32, name="y_codes", align_bytes=64)
-        y_plane = keep.tile([P, O], U8, name="y_plane", align_bytes=64)
+            nc.vector.tensor_copy(woven(y_rounded, half), in_runs(y, half))
+        y_codes = keep.tile([P, O], U32, name="y_codes", align_bytes=ALIGN)
+        y_plane = keep.tile([P, O], U8, name="y_plane", align_bytes=ALIGN)
         for half in HALVES:
             quantize(nc, y_codes, y_plane, y_rounded, half)
         nc.scalar.dma_start(
             out=out_1[0].rearrange("p c r -> p (c r)").bitcast(I32), in_=y_codes[:].bitcast(I32)
         )
-        for q in range(QUADS):
-            queue = nc.sync if q < 2 else nc.scalar
+        for quad, queue in enumerate((nc.sync, nc.sync, nc.scalar, nc.scalar)):
             queue.dma_start(
-                out=out_2[0, 4 * q : 4 * q + 4, :].bitcast(I32),
-                in_=y_plane[32 * q : 32 * q + 4, :].bitcast(I32),
+                out=out_2[0, PACK * quad : PACK * quad + PACK, :].bitcast(I32),
+                in_=y_plane[QUAD_ROWS * quad : QUAD_ROWS * quad + PACK, :].bitcast(I32),
             )

from contextlib import ExitStack

import concourse.mybir as mybir

K, T, J, R, O, N, E = 512, 2048, 256, 512, 128, 512, 1024
FLOPS = 2 * K * R * J * 2 + 2 * R * N * O

F32 = mybir.dt.float32
BF16 = mybir.dt.bfloat16
I32 = mybir.dt.int32
U32 = mybir.dt.uint32
U16 = mybir.dt.uint16
U8 = mybir.dt.uint8
E4M3 = mybir.dt.float8_e4m3fn_x4
E5M2 = mybir.dt.float8_e5m2_x4
E2M1 = mybir.dt.float4_e2m1fn_x4
ACT = mybir.ActivationFunctionType
ALU = mybir.AluOpType

P = 128
PACK = 4
QUADS = 4
QUAD_ROWS = P // QUADS
GROUP = 16
RUN = 4
ALIGN = 64
HALVES = (slice(0, O // 2), slice(O // 2, O))
SLICE_PAIRS = (slice(0, 2), slice(2, PACK))


def load_plane(queues, plane, rows):
    for quad in range(QUADS):
        queues[quad].dma_start(
            out=plane[QUAD_ROWS * quad : QUAD_ROWS * quad + PACK, :].bitcast(I32),
            in_=rows[0, PACK * quad : PACK * quad + PACK, :].bitcast(I32),
        )


def dealt(columns):
    return columns.rearrange("p (m t) -> p t m", t=PACK)


def slices(places):
    return places.rearrange("p (t m) -> p t m", t=PACK)


def entries(offsets, places):
    return offsets[:, places.start // GROUP : places.stop // GROUP]


def in_runs(by_slice, places):
    return by_slice[:, :, places].rearrange("p t (c i) -> p c t i", i=RUN)


def woven(by_place, places):
    return by_place[:, places, :].rearrange("p (c i) t -> p c t i", i=RUN)


def quantize(nc, codes, plane, rounded, places):
    nc.vector.quantize_mx(
        out=codes[:, places].bitcast(E4M3),
        scales=plane[:, places],
        in_=rounded[:, places, :].rearrange("p o t -> p (o t)"),
    )


def multiply(nc, acc, weight_codes, weight_plane, t, moving, moving_plane):
    nc.tensor.matmul_mx(
        out=acc[:],
        lhsT=weight_codes[:, 2 * P * t : 2 * P * (t + 1)].bitcast(E2M1),
        lhsT_scale=weight_plane[:, P * t : P * (t + 1)],
        rhs=moving,
        rhs_scale=moving_plane[:],
        start=True,
        stop=True,
    )


def tile_list_tied_looked_one_tabled_pl_kernel(
    tc, xt_words, xt_scales, w_words, w_scales, wb_words, wb_scales, tz,
    offs, offs2, offs3, offs4, offs5, out_0, out_1, out_2,
):
    nc = tc.nc
    with ExitStack() as ctx:
        lists = ctx.enter_context(tc.tile_pool(name="lists", bufs=1))
        keep = ctx.enter_context(tc.tile_pool(name="keep", bufs=1))
        psum = ctx.enter_context(tc.psum_pool(name="psum", bufs=1))

        tok_a = lists.tile([P, J // GROUP], U16, name="tok_a")
        tok_b = lists.tile([P, J // GROUP], U16, name="tok_b")
        slot_a = lists.tile([P, O // GROUP], U16, name="slot_a")
        slot_b = lists.tile([P, O // GROUP], U16, name="slot_b")
        entry = lists.tile([P, O // GROUP], U16, name="entry")

        x_words = keep.tile([P, T], U32, name="x_words", align_bytes=ALIGN)
        x_plane = keep.tile([P, T], U8, name="x_plane", align_bytes=ALIGN)
        w_raw = keep.tile([P, 2 * R], U8, name="w_raw", align_bytes=ALIGN)
        wb_raw = keep.tile([P, 2 * N], U8, name="wb_raw", align_bytes=ALIGN)
        w_plane_raw = keep.tile([P, R], U8, name="w_plane_raw", tag="w_plane_raw", align_bytes=ALIGN)
        wb_plane_raw = keep.tile([P, N], U8, name="wb_plane_raw", tag="wb_plane_raw", align_bytes=ALIGN)
        tz_rows = [keep.tile([P, 2, E], F32, name=f"tz_rows{pair}") for pair in range(2)]

        nc.vector.memset(x_plane[:].bitcast(I32), 0)
        nc.vector.memset(w_plane_raw[:].bitcast(I32), 0)
        nc.vector.memset(wb_plane_raw[:].bitcast(I32), 0)

        nc.sync.dma_start(tok_a[:], offs)
        nc.sync.dma_start(tok_b[:], offs2)
        nc.scalar.dma_start(out=w_raw[:].bitcast(I32), in_=w_words[0].bitcast(I32))
        load_plane((nc.sync, nc.scalar, nc.sync, nc.scalar), x_plane, xt_scales)
        nc.sync.dma_start(
            out=x_words[:].bitcast(I32),
            in_=xt_words[0].rearrange("p c r -> p (c r)").bitcast(I32),
        )
        load_plane([nc.sync] * QUADS, w_plane_raw, w_scales)
        nc.sync.dma_start(out=wb_raw[:].bitcast(I32), in_=wb_words[0].bitcast(I32))
        nc.sync.dma_start(slot_a[:], offs3)
        tz_by_slice = tz.rearrange("(p t) e -> p t e", t=PACK)
        nc.sync.dma_start(out=tz_rows[0][:], in_=tz_by_slice[:, SLICE_PAIRS[0], :])
        nc.sync.dma_start(slot_b[:], offs4)
        nc.sync.dma_start(entry[:], offs5)
        load_plane([nc.sync] * QUADS, wb_plane_raw, wb_scales)
        nc.sync.dma_start(out=tz_rows[1][:], in_=tz_by_slice[:, SLICE_PAIRS[1], :])

        xa_plane = keep.tile([P, J], U8, name="xa_plane", align_bytes=ALIGN)
        xb_plane = keep.tile([P, J], U8, name="xb_plane", align_bytes=ALIGN)
        xa_words = keep.tile([P, J], U32, name="xa_words", align_bytes=ALIGN)
        w_codes = keep.tile([P, 2 * R], U8, name="w_codes", align_bytes=ALIGN)
        w_plane = keep.tile([P, R], U8, name="w_plane", align_bytes=ALIGN)

        nc.vector.tensor_copy(slices(w_codes[:].bitcast(U16)), dealt(w_raw[:].bitcast(U16)))
        nc.vector.tensor_copy(xa_plane[:], x_plane[:].indirect(tok_a[:]))
        nc.vector.tensor_copy(xb_plane[:], x_plane[:].indirect(tok_b[:]))
        nc.vector.tensor_copy(xa_words[:], x_words[:].indirect(tok_a[:]))
        for pair in SLICE_PAIRS:
            nc.vector.tensor_copy(slices(w_plane[:])[:, pair, :], dealt(w_plane_raw[:])[:, pair, :])
        xb_words = keep.tile([P, J], U32, name="xb_words", tag="w_plane_raw", align_bytes=ALIGN)
        nc.vector.tensor_copy(xb_words[:], x_words[:].indirect(tok_b[:]))
        wb_codes = keep.tile([P, 2 * N], U8, name="wb_codes", align_bytes=ALIGN)
        nc.vector.tensor_copy(slices(wb_codes[:].bitcast(U16)), dealt(wb_raw[:].bitcast(U16)))

        def first_product(t, words, plane, bank, name):
            acc = psum.tile([P, J], F32, name=name + "_acc", tag=f"bank{bank}")
            multiply(nc, acc, w_codes, w_plane, t, words[:].bitcast(E5M2), plane)
            whole = keep.tile([P, J], F32, name=name, tag=name, align_bytes=ALIGN)
            nc.scalar.activation(whole[:], acc[:], ACT.Copy)
            return whole

        picked_a = keep.tile([P, PACK, O], F32, name="picked_a")
        diff = keep.tile([P, PACK, O], F32, name="diff", tag="diff")

        def product_a(t):
            return first_product(t, xa_words, xa_plane, t, f"a{t}")

        def product_b(t):
            return first_product(t, xb_words, xb_plane, PACK + t, f"b{t}")

        def subtract(t, b_rows, places):
            nc.vector.tensor_tensor(
                diff[:, t, places], b_rows[:].indirect(entries(slot_b, places)), picked_a[:, t, places], ALU.subtract
            )

        last = PACK - 1
        for t in range(last):
            nc.vector.tensor_copy(picked_a[:, t, :], product_a(t)[:].indirect(slot_a[:]))
        for t in range(last):
            subtract(t, product_b(t), slice(0, O))
        wb_plane = keep.tile([P, N], U8, name="wb_plane", align_bytes=ALIGN)
        a_last = product_a(last)
        b_last = product_b(last)
        for half in HALVES:
            nc.scalar.activation(picked_a[:, last, half], a_last[:].indirect(entries(slot_a, half)), ACT.Copy)
            subtract(last, b_last, half)

        hid = keep.tile([P, O, PACK], BF16, name="hid", tag="hid", align_bytes=ALIGN)
        for half in HALVES:
            nc.scalar.activation(woven(hid, half), in_runs(diff, half), ACT.Abs)
        nc.vector.tensor_copy(slices(wb_plane[:]), dealt(wb_plane_raw[:]))
        hid_codes = keep.tile([P, O], U32, name="hid_codes", tag="wb_plane_raw", align_bytes=ALIGN)
        hid_plane = keep.tile([P, O], U8, name="hid_plane", align_bytes=ALIGN)
        for half in HALVES:
            quantize(nc, hid_codes, hid_plane, hid, half)

        picked_z = [
            keep.tile([P, 2, O], F32, name="picked_z0", tag="hid", align_bytes=ALIGN),
            keep.tile([P, 2, O], F32, name="picked_z1", tag="diff"),
        ]
        for u in range(2):
            nc.vector.tensor_copy(picked_z[0][:, u, :], tz_rows[0][:, u, :].indirect(entry[:]))
            nc.scalar.activation(picked_z[1][:, u, :], tz_rows[1][:, u, :].indirect(entry[:]), ACT.Copy)

        y = keep.tile([P, PACK, O], F32, name="y")
        for t in range(PACK):
            acc = psum.tile([P, O], F32, name=f"p{t}_acc", tag=f"bank{t}")
            multiply(nc, acc, wb_codes, wb_plane, t, hid_codes[:].bitcast(E4M3), hid_plane)
            for places in HALVES if t == last else (slice(0, O),):
                nc.vector.tensor_tensor(y[:, t, places], acc[:, places], picked_z[t // 2][:, t % 2, places], ALU.add)
        nc.sync.dma_start(out=out_0.rearrange("(p t) o -> p t o", t=PACK), in_=y[:])

        y_rounded = keep.tile([P, O, PACK], BF16, name="y_rounded", align_bytes=ALIGN)
        for half in HALVES:
            nc.vector.tensor_copy(woven(y_rounded, half), in_runs(y, half))
        y_codes = keep.tile([P, O], U32, name="y_codes", align_bytes=ALIGN)
        y_plane = keep.tile([P, O], U8, name="y_plane", align_bytes=ALIGN)
        for half in HALVES:
            quantize(nc, y_codes, y_plane, y_rounded, half)
        nc.scalar.dma_start(
            out=out_1[0].rearrange("p c r -> p (c r)").bitcast(I32), in_=y_codes[:].bitcast(I32)
        )
        for quad, queue in enumerate((nc.sync, nc.sync, nc.scalar, nc.scalar)):
            queue.dma_start(
                out=out_2[0, PACK * quad : PACK * quad + PACK, :].bitcast(I32),
                in_=y_plane[QUAD_ROWS * quad : QUAD_ROWS * quad + PACK, :].bitcast(I32),
            )
